import numpy as np
import ml_dtypes

BF16 = ml_dtypes.bfloat16


def bf(x):
    return np.asarray(x, np.float32).astype(BF16)


def f32(x):
    return np.asarray(x, np.float32)


def f64(x):
    return np.asarray(x).astype(np.float64)


def striped(idx):
    return np.concatenate([l.reshape(-1, 16).T for l in idx])


def rows(idx, k):
    return np.tile(np.repeat(idx, 16, axis=0), (k // (16 * 8), 1))


def look(tab, idx):
    return np.take_along_axis(f64(tab), rows(idx, len(tab)), axis=1)


K, S, V, N = 256, 2048, 1536, 1536


def silu(v):
    return v / (1.0 + np.exp(-v))


def setup_inputs():
    return {"tab": f32(np.random.standard_normal((2, K, S))), "offs": striped(np.stack([np.random.permutation(S)[:N] for _ in range(8)]))}


def reference(tab, offs):
    idx = np.stack([g.T.reshape(-1) for g in np.split(offs, 8)])
    x = ((look(tab[0], idx) - 0.125) * 1.5) * (silu(look(tab[1], idx)))
    return x

@@ -1,0 +1,58 @@
+import concourse.mybir as mybir
+
+F32 = mybir.dt.float32
+U16 = mybir.dt.uint16
+ALU = mybir.AluOpType
+SILU = mybir.ActivationFunctionType.Silu
+
+P = 128
+PIECE = 512
+OFFSETS_PER_COLUMN = 16
+
+
+def tile_lookup_vg_nrmsilu_out_kernel(tc, tab, offs, out):
+    nc = tc.nc
+    _, rows, places = tab.shape
+    n = out.shape[1]
+    blocks = rows // P
+    pieces = n // PIECE
+    piece_columns = PIECE // OFFSETS_PER_COLUMN
+
+    with (
+        tc.tile_pool(name="held", bufs=1) as held,
+        tc.tile_pool(name="work", bufs=blocks * pieces) as work,
+    ):
+        zeros = held.tile([P, 1], F32, name="zeros")
+        nc.vector.memset(zeros[:], 0.0)
+        warm = held.tile([P, 1], F32, name="warm")
+        nc.scalar.activation(warm[:], zeros[:], SILU)
+
+        lists = held.tile([P, n // OFFSETS_PER_COLUMN], U16, name="lists")
+        nc.sync.dma_start(lists[:], offs)
+
+        value_tables = []
+        gate_tables = []
+        for b in range(blocks):
+            block_rows = slice(b * P, (b + 1) * P)
+            value_table = held.tile([P, places], F32, name=f"value_table{b}")
+            nc.sync.dma_start(value_table[:], tab[0, block_rows, :])
+            value_tables.append(value_table)
+            gate_table = held.tile([P, places], F32, name=f"gate_table{b}")
+            nc.sync.dma_start(gate_table[:], tab[1, block_rows, :])
+            gate_tables.append(gate_table)
+
+        for b in range(blocks):
+            for k in range(pieces):
+                piece_list = lists[:, k * piece_columns : (k + 1) * piece_columns]
+
+                value = work.tile([P, PIECE], F32, name="value")
+                nc.vector.tensor_scalar(
+                    value[:], value_tables[b][:].indirect(piece_list), 0.125, 1.5, ALU.subtract, ALU.mult
+                )
+                gate = work.tile([P, PIECE], F32, name="gate")
+                nc.scalar.activation(gate[:], gate_tables[b][:].indirect(piece_list), SILU)
+
+                product = work.tile([P, PIECE], F32, name="product")
+                product_engine = nc.vector if b == blocks - 1 else nc.gpsimd
+                product_engine.tensor_tensor(product[:], value[:], gate[:], ALU.mult)
+                nc.sync.dma_start(out[b * P : (b + 1) * P, k * PIECE : (k + 1) * PIECE], product[:])

@@ -7,6 +7,7 @@ SILU = mybir.ActivationFunctionType.Silu
 
 P = 128
 PIECE = 512
+FIRST_CHUNK = 256
 OFFSETS_PER_COLUMN = 16
 
 
@@ -54,5 +55,8 @@ def tile_lookup_vg_nrmsilu_out_kernel(tc, tab, offs, out):
 
                 product = work.tile([P, PIECE], F32, name="product")
                 product_engine = nc.vector if b == blocks - 1 else nc.gpsimd
-                product_engine.tensor_tensor(product[:], value[:], gate[:], ALU.mult)
-                nc.sync.dma_start(out[b * P : (b + 1) * P, k * PIECE : (k + 1) * PIECE], product[:])
+                is_last = b == blocks - 1 and k == pieces - 1
+                cuts = [0, FIRST_CHUNK, PIECE] if is_last else [0, PIECE]
+                for lo, hi in zip(cuts, cuts[1:]):
+                    product_engine.tensor_tensor(product[:, lo:hi], value[:, lo:hi], gate[:, lo:hi], ALU.mult)
+                    nc.sync.dma_start(out[b * P : (b + 1) * P, k * PIECE + lo : k * PIECE + hi], product[:, lo:hi])

@@ -7,8 +7,8 @@ SILU = mybir.ActivationFunctionType.Silu
 
 P = 128
 PIECE = 512
-FIRST_CHUNK = 256
 OFFSETS_PER_COLUMN = 16
+LAST_CUTS = [0, 128, 256, 512]
 
 
 def tile_lookup_vg_nrmsilu_out_kernel(tc, tab, offs, out):
@@ -54,9 +54,13 @@ def tile_lookup_vg_nrmsilu_out_kernel(tc, tab, offs, out):
                 nc.scalar.activation(gate[:], gate_tables[b][:].indirect(piece_list), SILU)
 
                 product = work.tile([P, PIECE], F32, name="product")
-                product_engine = nc.vector if b == blocks - 1 else nc.gpsimd
-                is_last = b == blocks - 1 and k == pieces - 1
-                cuts = [0, FIRST_CHUNK, PIECE] if is_last else [0, PIECE]
-                for lo, hi in zip(cuts, cuts[1:]):
-                    product_engine.tensor_tensor(product[:, lo:hi], value[:, lo:hi], gate[:, lo:hi], ALU.mult)
-                    nc.sync.dma_start(out[b * P : (b + 1) * P, k * PIECE + lo : k * PIECE + hi], product[:, lo:hi])
+                piece_out = out[b * P : (b + 1) * P, k * PIECE : (k + 1) * PIECE]
+                if b < blocks - 1:
+                    nc.gpsimd.tensor_tensor(product[:], value[:], gate[:], ALU.mult)
+                    for lo in range(0, PIECE, PIECE // 2):
+                        nc.sync.dma_start(piece_out[:, lo : lo + PIECE // 2], product[:, lo : lo + PIECE // 2])
+                else:
+                    cuts = LAST_CUTS if k == pieces - 1 else [0, PIECE]
+                    for lo, hi in zip(cuts, cuts[1:]):
+                        nc.vector.tensor_tensor(product[:, lo:hi], value[:, lo:hi], gate[:, lo:hi], ALU.mult)
+                        nc.sync.dma_start(piece_out[:, lo:hi], product[:, lo:hi])

@@ -8,7 +8,7 @@ SILU = mybir.ActivationFunctionType.Silu
 P = 128
 PIECE = 512
 OFFSETS_PER_COLUMN = 16
-LAST_CUTS = [0, 128, 256, 512]
+LAST_CUTS = [0, 128, 320, 512]
 
 
 def tile_lookup_vg_nrmsilu_out_kernel(tc, tab, offs, out):

@@ -29,7 +29,6 @@ def tile_lookup_vg_nrmsilu_out_kernel(tc, tab, offs, out):
         nc.scalar.activation(warm[:], zeros[:], SILU)
 
         lists = held.tile([P, n // OFFSETS_PER_COLUMN], U16, name="lists")
-        nc.sync.dma_start(lists[:], offs)
 
         value_tables = []
         gate_tables = []
@@ -38,6 +37,8 @@ def tile_lookup_vg_nrmsilu_out_kernel(tc, tab, offs, out):
             value_table = held.tile([P, places], F32, name=f"value_table{b}")
             nc.sync.dma_start(value_table[:], tab[0, block_rows, :])
             value_tables.append(value_table)
+            if b == 0:
+                nc.sync.dma_start(lists[:], offs)
             gate_table = held.tile([P, places], F32, name=f"gate_table{b}")
             nc.sync.dma_start(gate_table[:], tab[1, block_rows, :])
             gate_tables.append(gate_table)

@@ -1,4 +1,5 @@
 import concourse.mybir as mybir
+from concourse.masks import make_identity
 
 F32 = mybir.dt.float32
 U16 = mybir.dt.uint16
@@ -8,7 +9,9 @@ SILU = mybir.ActivationFunctionType.Silu
 P = 128
 PIECE = 512
 OFFSETS_PER_COLUMN = 16
-LAST_CUTS = [0, 128, 320, 512]
+HALF = PIECE // 2
+FIRST = 144
+ON_VECTOR = 368
 
 
 def tile_lookup_vg_nrmsilu_out_kernel(tc, tab, offs, out):
@@ -22,14 +25,17 @@ def tile_lookup_vg_nrmsilu_out_kernel(tc, tab, offs, out):
     with (
         tc.tile_pool(name="held", bufs=1) as held,
         tc.tile_pool(name="work", bufs=blocks * pieces) as work,
+        tc.psum_pool(name="psum", bufs=1) as psum,
     ):
         zeros = held.tile([P, 1], F32, name="zeros")
         nc.vector.memset(zeros[:], 0.0)
         warm = held.tile([P, 1], F32, name="warm")
         nc.scalar.activation(warm[:], zeros[:], SILU)
 
-        lists = held.tile([P, n // OFFSETS_PER_COLUMN], U16, name="lists")
+        identity = held.tile([P, P], F32, name="identity")
+        make_identity(nc, identity[:])
 
+        lists = held.tile([P, n // OFFSETS_PER_COLUMN], U16, name="lists")
         value_tables = []
         gate_tables = []
         for b in range(blocks):
@@ -43,25 +49,37 @@ def tile_lookup_vg_nrmsilu_out_kernel(tc, tab, offs, out):
             nc.sync.dma_start(gate_table[:], tab[1, block_rows, :])
             gate_tables.append(gate_table)
 
-        for b in range(blocks):
-            for k in range(pieces):
-                piece_list = lists[:, k * piece_columns : (k + 1) * piece_columns]
+        def piece_list(k):
+            return lists[:, k * piece_columns : (k + 1) * piece_columns]
 
-                value = work.tile([P, PIECE], F32, name="value")
+        for b in range(blocks):
+            value_order = [pieces - 1, *range(pieces - 1)] if b == blocks - 1 else range(pieces)
+            values = {}
+            for k in value_order:
+                values[k] = work.tile([P, PIECE], F32, name="value")
                 nc.vector.tensor_scalar(
-                    value[:], value_tables[b][:].indirect(piece_list), 0.125, 1.5, ALU.subtract, ALU.mult
+                    values[k][:], value_tables[b][:].indirect(piece_list(k)), 0.125, 1.5, ALU.subtract, ALU.mult
                 )
+            for k in range(pieces):
+                value = values[k]
                 gate = work.tile([P, PIECE], F32, name="gate")
-                nc.scalar.activation(gate[:], gate_tables[b][:].indirect(piece_list), SILU)
+                nc.scalar.activation(gate[:], gate_tables[b][:].indirect(piece_list(k)), SILU)
 
                 product = work.tile([P, PIECE], F32, name="product")
                 piece_out = out[b * P : (b + 1) * P, k * PIECE : (k + 1) * PIECE]
-                if b < blocks - 1:
-                    nc.gpsimd.tensor_tensor(product[:], value[:], gate[:], ALU.mult)
-                    for lo in range(0, PIECE, PIECE // 2):
-                        nc.sync.dma_start(piece_out[:, lo : lo + PIECE // 2], product[:, lo : lo + PIECE // 2])
+                if b == blocks - 1 and k == pieces - 1:
+                    moved = psum.tile([P, ON_VECTOR], F32, name="moved")
+                    nc.tensor.matmul(moved[:], identity[:], value[:, :ON_VECTOR], start=True, stop=True)
+                    nc.vector.tensor_tensor(product[:, :FIRST], moved[:, :FIRST], gate[:, :FIRST], ALU.mult)
+                    nc.sync.dma_start(piece_out[:, :FIRST], product[:, :FIRST])
+                    nc.gpsimd.tensor_tensor(product[:, ON_VECTOR:], value[:, ON_VECTOR:], gate[:, ON_VECTOR:], ALU.mult)
+                    nc.vector.tensor_tensor(
+                        product[:, FIRST:ON_VECTOR], moved[:, FIRST:], gate[:, FIRST:ON_VECTOR], ALU.mult
+                    )
+                    nc.sync.dma_start(piece_out[:, FIRST:], product[:, FIRST:])
                 else:
-                    cuts = LAST_CUTS if k == pieces - 1 else [0, PIECE]
-                    for lo, hi in zip(cuts, cuts[1:]):
-                        nc.vector.tensor_tensor(product[:, lo:hi], value[:, lo:hi], gate[:, lo:hi], ALU.mult)
-                        nc.sync.dma_start(piece_out[:, lo:hi], product[:, lo:hi])
+                    product_engine = nc.vector if b == blocks - 1 else nc.gpsimd
+                    product_engine.tensor_tensor(product[:], value[:], gate[:], ALU.mult)
+                    width = PIECE if b == blocks - 1 and k == pieces - 2 else HALF
+                    for lo in range(0, PIECE, width):
+                        nc.sync.dma_start(piece_out[:, lo : lo + width], product[:, lo : lo + width])

@@ -12,74 +12,79 @@ OFFSETS_PER_COLUMN = 16
 HALF = PIECE // 2
 FIRST = 144
 ON_VECTOR = 368
+EARLY_ON_GPSIMD = 448
 
 
 def tile_lookup_vg_nrmsilu_out_kernel(tc, tab, offs, out):
     nc = tc.nc
-    _, rows, places = tab.shape
+    places = tab.shape[2]
     n = out.shape[1]
-    blocks = rows // P
-    pieces = n // PIECE
-    piece_columns = PIECE // OFFSETS_PER_COLUMN
+    pieces = [slice(lo, lo + PIECE) for lo in range(0, n, PIECE)]
 
     with (
         tc.tile_pool(name="held", bufs=1) as held,
-        tc.tile_pool(name="work", bufs=blocks * pieces) as work,
         tc.psum_pool(name="psum", bufs=1) as psum,
     ):
-        zeros = held.tile([P, 1], F32, name="zeros")
-        nc.vector.memset(zeros[:], 0.0)
-        warm = held.tile([P, 1], F32, name="warm")
-        nc.scalar.activation(warm[:], zeros[:], SILU)
-
         identity = held.tile([P, P], F32, name="identity")
         make_identity(nc, identity[:])
 
+        def load(which, block):
+            table = held.tile([P, places], F32, name=f"table{which}_{block}")
+            nc.sync.dma_start(table[:], tab[which, block * P : (block + 1) * P, :])
+            return table
+
+        gate_table0 = load(1, 0)
         lists = held.tile([P, n // OFFSETS_PER_COLUMN], U16, name="lists")
-        value_tables = []
-        gate_tables = []
-        for b in range(blocks):
-            block_rows = slice(b * P, (b + 1) * P)
-            value_table = held.tile([P, places], F32, name=f"value_table{b}")
-            nc.sync.dma_start(value_table[:], tab[0, block_rows, :])
-            value_tables.append(value_table)
-            if b == 0:
-                nc.sync.dma_start(lists[:], offs)
-            gate_table = held.tile([P, places], F32, name=f"gate_table{b}")
-            nc.sync.dma_start(gate_table[:], tab[1, block_rows, :])
-            gate_tables.append(gate_table)
+        nc.sync.dma_start(lists[:], offs)
+        value_table0 = load(0, 0)
+        value_table1 = load(0, 1)
+        gate_table1 = load(1, 1)
 
-        def piece_list(k):
-            return lists[:, k * piece_columns : (k + 1) * piece_columns]
+        def entries(piece):
+            return lists[:, piece.start // OFFSETS_PER_COLUMN : piece.stop // OFFSETS_PER_COLUMN]
 
-        for b in range(blocks):
-            value_order = [pieces - 1, *range(pieces - 1)] if b == blocks - 1 else range(pieces)
-            values = {}
-            for k in value_order:
-                values[k] = work.tile([P, PIECE], F32, name="value")
+        def look_up_values(table, order, name):
+            value = held.tile([P, n], F32, name=name)
+            for piece in order:
                 nc.vector.tensor_scalar(
-                    values[k][:], value_tables[b][:].indirect(piece_list(k)), 0.125, 1.5, ALU.subtract, ALU.mult
+                    value[:, piece], table[:].indirect(entries(piece)), 0.125, 1.5, ALU.subtract, ALU.mult
                 )
-            for k in range(pieces):
-                value = values[k]
-                gate = work.tile([P, PIECE], F32, name="gate")
-                nc.scalar.activation(gate[:], gate_tables[b][:].indirect(piece_list(k)), SILU)
+            return value
 
-                product = work.tile([P, PIECE], F32, name="product")
-                piece_out = out[b * P : (b + 1) * P, k * PIECE : (k + 1) * PIECE]
-                if b == blocks - 1 and k == pieces - 1:
-                    moved = psum.tile([P, ON_VECTOR], F32, name="moved")
-                    nc.tensor.matmul(moved[:], identity[:], value[:, :ON_VECTOR], start=True, stop=True)
-                    nc.vector.tensor_tensor(product[:, :FIRST], moved[:, :FIRST], gate[:, :FIRST], ALU.mult)
-                    nc.sync.dma_start(piece_out[:, :FIRST], product[:, :FIRST])
-                    nc.gpsimd.tensor_tensor(product[:, ON_VECTOR:], value[:, ON_VECTOR:], gate[:, ON_VECTOR:], ALU.mult)
-                    nc.vector.tensor_tensor(
-                        product[:, FIRST:ON_VECTOR], moved[:, FIRST:], gate[:, FIRST:ON_VECTOR], ALU.mult
-                    )
-                    nc.sync.dma_start(piece_out[:, FIRST:], product[:, FIRST:])
-                else:
-                    product_engine = nc.vector if b == blocks - 1 else nc.gpsimd
-                    product_engine.tensor_tensor(product[:], value[:], gate[:], ALU.mult)
-                    width = PIECE if b == blocks - 1 and k == pieces - 2 else HALF
-                    for lo in range(0, PIECE, width):
-                        nc.sync.dma_start(piece_out[:, lo : lo + width], product[:, lo : lo + width])
+        def look_up_gates(table, name):
+            gate = held.tile([P, n], F32, name=name)
+            for piece in pieces:
+                nc.scalar.activation(gate[:, piece], table[:].indirect(entries(piece)), SILU)
+            return gate
+
+        gate = look_up_gates(gate_table0, "gate0")
+        value = look_up_values(value_table0, pieces, "value0")
+        product = held.tile([P, n], F32, name="product0")
+        for piece in pieces:
+            nc.gpsimd.tensor_tensor(product[:, piece], value[:, piece], gate[:, piece], ALU.mult)
+        for lo in range(0, n, HALF):
+            nc.sync.dma_start(out[:P, lo : lo + HALF], product[:, lo : lo + HALF])
+
+        value = look_up_values(value_table1, pieces[-1:] + pieces[:-1], "value1")
+        gate = look_up_gates(gate_table1, "gate1")
+        product = held.tile([P, n], F32, name="product1")
+        last = n - PIECE
+        moved = psum.tile([P, ON_VECTOR], F32, name="moved")
+        nc.tensor.matmul(moved[:], identity[:], value[:, last : last + ON_VECTOR], start=True, stop=True)
+        middle = (EARLY_ON_GPSIMD + last) // 2
+        for engine, lo, hi in [
+            (nc.gpsimd, 0, EARLY_ON_GPSIMD),
+            (nc.vector, EARLY_ON_GPSIMD, middle),
+            (nc.vector, middle, last),
+        ]:
+            engine.tensor_tensor(product[:, lo:hi], value[:, lo:hi], gate[:, lo:hi], ALU.mult)
+            nc.sync.dma_start(out[P:, lo:hi], product[:, lo:hi])
+
+        first = slice(last, last + FIRST)
+        nc.vector.tensor_tensor(product[:, first], moved[:, :FIRST], gate[:, first], ALU.mult)
+        nc.sync.dma_start(out[P:, first], product[:, first])
+        on_gpsimd = slice(last + ON_VECTOR, n)
+        nc.gpsimd.tensor_tensor(product[:, on_gpsimd], value[:, on_gpsimd], gate[:, on_gpsimd], ALU.mult)
+        on_vector = slice(last + FIRST, last + ON_VECTOR)
+        nc.vector.tensor_tensor(product[:, on_vector], moved[:, FIRST:], gate[:, on_vector], ALU.mult)
+        nc.sync.dma_start(out[P:, last + FIRST :], product[:, last + FIRST :])

@@ -1,5 +1,4 @@
 import concourse.mybir as mybir
-from concourse.masks import make_identity
 
 F32 = mybir.dt.float32
 U16 = mybir.dt.uint16
@@ -10,9 +9,7 @@ P = 128
 PIECE = 512
 OFFSETS_PER_COLUMN = 16
 HALF = PIECE // 2
-FIRST = 144
-ON_VECTOR = 368
-EARLY_ON_GPSIMD = 448
+FIRST = 224
 
 
 def tile_lookup_vg_nrmsilu_out_kernel(tc, tab, offs, out):
@@ -21,13 +18,7 @@ def tile_lookup_vg_nrmsilu_out_kernel(tc, tab, offs, out):
     n = out.shape[1]
     pieces = [slice(lo, lo + PIECE) for lo in range(0, n, PIECE)]
 
-    with (
-        tc.tile_pool(name="held", bufs=1) as held,
-        tc.psum_pool(name="psum", bufs=1) as psum,
-    ):
-        identity = held.tile([P, P], F32, name="identity")
-        make_identity(nc, identity[:])
-
+    with tc.tile_pool(name="held", bufs=1) as held:
         def load(which, block):
             table = held.tile([P, places], F32, name=f"table{which}_{block}")
             nc.sync.dma_start(table[:], tab[which, block * P : (block + 1) * P, :])
@@ -43,9 +34,9 @@ def tile_lookup_vg_nrmsilu_out_kernel(tc, tab, offs, out):
         def entries(piece):
             return lists[:, piece.start // OFFSETS_PER_COLUMN : piece.stop // OFFSETS_PER_COLUMN]
 
-        def look_up_values(table, order, name):
+        def look_up_values(table, name):
             value = held.tile([P, n], F32, name=name)
-            for piece in order:
+            for piece in pieces:
                 nc.vector.tensor_scalar(
                     value[:, piece], table[:].indirect(entries(piece)), 0.125, 1.5, ALU.subtract, ALU.mult
                 )
@@ -58,33 +49,21 @@ def tile_lookup_vg_nrmsilu_out_kernel(tc, tab, offs, out):
             return gate
 
         gate = look_up_gates(gate_table0, "gate0")
-        value = look_up_values(value_table0, pieces, "value0")
+        value = look_up_values(value_table0, "value0")
         product = held.tile([P, n], F32, name="product0")
         for piece in pieces:
             nc.gpsimd.tensor_tensor(product[:, piece], value[:, piece], gate[:, piece], ALU.mult)
         for lo in range(0, n, HALF):
             nc.sync.dma_start(out[:P, lo : lo + HALF], product[:, lo : lo + HALF])
 
-        value = look_up_values(value_table1, pieces[-1:] + pieces[:-1], "value1")
+        value = look_up_values(value_table1, "value1")
         gate = look_up_gates(gate_table1, "gate1")
         product = held.tile([P, n], F32, name="product1")
-        last = n - PIECE
-        moved = psum.tile([P, ON_VECTOR], F32, name="moved")
-        nc.tensor.matmul(moved[:], identity[:], value[:, last : last + ON_VECTOR], start=True, stop=True)
-        middle = (EARLY_ON_GPSIMD + last) // 2
-        for engine, lo, hi in [
-            (nc.gpsimd, 0, EARLY_ON_GPSIMD),
-            (nc.vector, EARLY_ON_GPSIMD, middle),
-            (nc.vector, middle, last),
-        ]:
-            engine.tensor_tensor(product[:, lo:hi], value[:, lo:hi], gate[:, lo:hi], ALU.mult)
-            nc.sync.dma_start(out[P:, lo:hi], product[:, lo:hi])
-
-        first = slice(last, last + FIRST)
-        nc.vector.tensor_tensor(product[:, first], moved[:, :FIRST], gate[:, first], ALU.mult)
+        first = pieces[0]
+        nc.gpsimd.tensor_tensor(product[:, first], value[:, first], gate[:, first], ALU.mult)
         nc.sync.dma_start(out[P:, first], product[:, first])
-        on_gpsimd = slice(last + ON_VECTOR, n)
-        nc.gpsimd.tensor_tensor(product[:, on_gpsimd], value[:, on_gpsimd], gate[:, on_gpsimd], ALU.mult)
-        on_vector = slice(last + FIRST, last + ON_VECTOR)
-        nc.vector.tensor_tensor(product[:, on_vector], moved[:, FIRST:], gate[:, on_vector], ALU.mult)
-        nc.sync.dma_start(out[P:, last + FIRST :], product[:, last + FIRST :])
+        for piece in pieces[1:]:
+            cut = piece.start + FIRST
+            for chunk in [slice(piece.start, cut), slice(cut, piece.stop)]:
+                nc.vector.tensor_tensor(product[:, chunk], value[:, chunk], gate[:, chunk], ALU.mult)
+                nc.sync.dma_start(out[P:, chunk], product[:, chunk])

@@ -9,6 +9,7 @@ P = 128
 PIECE = 512
 OFFSETS_PER_COLUMN = 16
 HALF = PIECE // 2
+BURST_BYTES = 256
 FIRST = 224
 
 
@@ -20,12 +21,12 @@ def tile_lookup_vg_nrmsilu_out_kernel(tc, tab, offs, out):
 
     with tc.tile_pool(name="held", bufs=1) as held:
         def load(which, block):
-            table = held.tile([P, places], F32, name=f"table{which}_{block}")
+            table = held.tile([P, places], F32, name=f"table{which}_{block}", align_bytes=BURST_BYTES)
             nc.sync.dma_start(table[:], tab[which, block * P : (block + 1) * P, :])
             return table
 
         gate_table0 = load(1, 0)
-        lists = held.tile([P, n // OFFSETS_PER_COLUMN], U16, name="lists")
+        lists = held.tile([P, n // OFFSETS_PER_COLUMN], U16, name="lists", align_bytes=BURST_BYTES)
         nc.sync.dma_start(lists[:], offs)
         value_table0 = load(0, 0)
         value_table1 = load(0, 1)
@@ -50,7 +51,7 @@ def tile_lookup_vg_nrmsilu_out_kernel(tc, tab, offs, out):
 
         gate = look_up_gates(gate_table0, "gate0")
         value = look_up_values(value_table0, "value0")
-        product = held.tile([P, n], F32, name="product0")
+        product = held.tile([P, n], F32, name="product0", align_bytes=BURST_BYTES)
         for piece in pieces:
             nc.gpsimd.tensor_tensor(product[:, piece], value[:, piece], gate[:, piece], ALU.mult)
         for lo in range(0, n, HALF):
@@ -58,7 +59,7 @@ def tile_lookup_vg_nrmsilu_out_kernel(tc, tab, offs, out):
 
         value = look_up_values(value_table1, "value1")
         gate = look_up_gates(gate_table1, "gate1")
-        product = held.tile([P, n], F32, name="product1")
+        product = held.tile([P, n], F32, name="product1", align_bytes=BURST_BYTES)
         first = pieces[0]
         nc.gpsimd.tensor_tensor(product[:, first], value[:, first], gate[:, first], ALU.mult)
         nc.sync.dma_start(out[P:, first], product[:, first])

@@ -1,4 +1,5 @@
 import concourse.mybir as mybir
+from concourse.masks import make_identity
 
 F32 = mybir.dt.float32
 U16 = mybir.dt.uint16
@@ -10,16 +11,17 @@ PIECE = 512
 OFFSETS_PER_COLUMN = 16
 HALF = PIECE // 2
 BURST_BYTES = 256
-FIRST = 224
+FIRST = 160
+ON_GPSIMD = 384
 
 
 def tile_lookup_vg_nrmsilu_out_kernel(tc, tab, offs, out):
     nc = tc.nc
     places = tab.shape[2]
     n = out.shape[1]
-    pieces = [slice(lo, lo + PIECE) for lo in range(0, n, PIECE)]
+    first, middle, last = [slice(lo, lo + PIECE) for lo in range(0, n, PIECE)]
 
-    with tc.tile_pool(name="held", bufs=1) as held:
+    with tc.tile_pool(name="held", bufs=1) as held, tc.psum_pool(name="psum", bufs=1) as psum:
         def load(which, block):
             table = held.tile([P, places], F32, name=f"table{which}_{block}", align_bytes=BURST_BYTES)
             nc.sync.dma_start(table[:], tab[which, block * P : (block + 1) * P, :])
@@ -29,13 +31,16 @@ def tile_lookup_vg_nrmsilu_out_kernel(tc, tab, offs, out):
         lists = held.tile([P, n // OFFSETS_PER_COLUMN], U16, name="lists", align_bytes=BURST_BYTES)
         nc.sync.dma_start(lists[:], offs)
         value_table0 = load(0, 0)
-        value_table1 = load(0, 1)
         gate_table1 = load(1, 1)
+        value_table1 = load(0, 1)
+
+        identity = held.tile([P, P], F32, name="identity")
+        make_identity(nc, identity[:])
 
         def entries(piece):
             return lists[:, piece.start // OFFSETS_PER_COLUMN : piece.stop // OFFSETS_PER_COLUMN]
 
-        def look_up_values(table, name):
+        def look_up_values(table, name, pieces):
             value = held.tile([P, n], F32, name=name)
             for piece in pieces:
                 nc.vector.tensor_scalar(
@@ -43,28 +48,40 @@ def tile_lookup_vg_nrmsilu_out_kernel(tc, tab, offs, out):
                 )
             return value
 
-        def look_up_gates(table, name):
+        def look_up_gates(table, name, pieces):
             gate = held.tile([P, n], F32, name=name)
             for piece in pieces:
                 nc.scalar.activation(gate[:, piece], table[:].indirect(entries(piece)), SILU)
             return gate
 
-        gate = look_up_gates(gate_table0, "gate0")
-        value = look_up_values(value_table0, "value0")
+        gate = look_up_gates(gate_table0, "gate0", [first, middle, last])
+        value = look_up_values(value_table0, "value0", [first, middle, last])
         product = held.tile([P, n], F32, name="product0", align_bytes=BURST_BYTES)
-        for piece in pieces:
+        for piece in [first, middle, last]:
             nc.gpsimd.tensor_tensor(product[:, piece], value[:, piece], gate[:, piece], ALU.mult)
         for lo in range(0, n, HALF):
             nc.sync.dma_start(out[:P, lo : lo + HALF], product[:, lo : lo + HALF])
 
-        value = look_up_values(value_table1, "value1")
-        gate = look_up_gates(gate_table1, "gate1")
+        gate = look_up_gates(gate_table1, "gate1", [last, first, middle])
+        cut = middle.start + ON_GPSIMD
+        moved = []
+        for k, columns in enumerate([last, slice(cut, middle.stop)]):
+            bank = psum.tile([P, columns.stop - columns.start], F32, name=f"moved_gate{k}")
+            nc.tensor.matmul(bank[:], identity[:], gate[:, columns], start=True, stop=True)
+            moved.append(bank)
+        last_gate, middle_gate = moved
+        value = look_up_values(value_table1, "value1", [first, middle, last])
         product = held.tile([P, n], F32, name="product1", align_bytes=BURST_BYTES)
-        first = pieces[0]
         nc.gpsimd.tensor_tensor(product[:, first], value[:, first], gate[:, first], ALU.mult)
-        nc.sync.dma_start(out[P:, first], product[:, first])
-        for piece in pieces[1:]:
-            cut = piece.start + FIRST
-            for chunk in [slice(piece.start, cut), slice(cut, piece.stop)]:
-                nc.vector.tensor_tensor(product[:, chunk], value[:, chunk], gate[:, chunk], ALU.mult)
-                nc.sync.dma_start(out[P:, chunk], product[:, chunk])
+        for lo in range(0, PIECE, HALF):
+            nc.sync.dma_start(out[P:, lo : lo + HALF], product[:, lo : lo + HALF])
+        chunk = slice(middle.start, cut)
+        nc.gpsimd.tensor_tensor(product[:, chunk], value[:, chunk], gate[:, chunk], ALU.mult)
+        nc.sync.dma_start(out[P:, chunk], product[:, chunk])
+        chunk = slice(cut, middle.stop)
+        nc.vector.tensor_tensor(product[:, chunk], value[:, chunk], middle_gate[:], ALU.mult)
+        for lo, hi in [(0, FIRST), (FIRST, PIECE)]:
+            chunk = slice(last.start + lo, last.start + hi)
+            nc.vector.tensor_tensor(product[:, chunk], value[:, chunk], last_gate[:, lo:hi], ALU.mult)
+        for chunk in [slice(cut, last.start + FIRST), slice(last.start + FIRST, n)]:
+            nc.sync.dma_start(out[P:, chunk], product[:, chunk])

@@ -11,8 +11,7 @@ PIECE = 512
 OFFSETS_PER_COLUMN = 16
 HALF = PIECE // 2
 BURST_BYTES = 256
-FIRST = 160
-ON_GPSIMD = 384
+ON_GPSIMD = 320
 
 
 def tile_lookup_vg_nrmsilu_out_kernel(tc, tab, offs, out):
@@ -22,6 +21,10 @@ def tile_lookup_vg_nrmsilu_out_kernel(tc, tab, offs, out):
     first, middle, last = [slice(lo, lo + PIECE) for lo in range(0, n, PIECE)]
 
     with tc.tile_pool(name="held", bufs=1) as held, tc.psum_pool(name="psum", bufs=1) as psum:
+        unused = held.tile([P, 1], F32, name="unused")
+        nc.vector.memset(unused[:], 0.0)
+        nc.scalar.activation(unused[:], unused[:], SILU)
+
         def load(which, block):
             table = held.tile([P, places], F32, name=f"table{which}_{block}", align_bytes=BURST_BYTES)
             nc.sync.dma_start(table[:], tab[which, block * P : (block + 1) * P, :])
@@ -64,24 +67,26 @@ def tile_lookup_vg_nrmsilu_out_kernel(tc, tab, offs, out):
 
         gate = look_up_gates(gate_table1, "gate1", [last, first, middle])
         cut = middle.start + ON_GPSIMD
-        moved = []
-        for k, columns in enumerate([last, slice(cut, middle.stop)]):
-            bank = psum.tile([P, columns.stop - columns.start], F32, name=f"moved_gate{k}")
-            nc.tensor.matmul(bank[:], identity[:], gate[:, columns], start=True, stop=True)
-            moved.append(bank)
-        last_gate, middle_gate = moved
+        moved_gate = psum.tile([P, 2 * PIECE], F32, name="moved_gate")
+        for columns in [last, slice(cut, last.start)]:
+            into = moved_gate[:, columns.start - middle.start : columns.stop - middle.start]
+            nc.tensor.matmul(into, identity[:], gate[:, columns], start=True, stop=True)
         value = look_up_values(value_table1, "value1", [first, middle, last])
         product = held.tile([P, n], F32, name="product1", align_bytes=BURST_BYTES)
-        nc.gpsimd.tensor_tensor(product[:, first], value[:, first], gate[:, first], ALU.mult)
-        for lo in range(0, PIECE, HALF):
-            nc.sync.dma_start(out[P:, lo : lo + HALF], product[:, lo : lo + HALF])
-        chunk = slice(middle.start, cut)
-        nc.gpsimd.tensor_tensor(product[:, chunk], value[:, chunk], gate[:, chunk], ALU.mult)
-        nc.sync.dma_start(out[P:, chunk], product[:, chunk])
-        chunk = slice(cut, middle.stop)
-        nc.vector.tensor_tensor(product[:, chunk], value[:, chunk], middle_gate[:], ALU.mult)
-        for lo, hi in [(0, FIRST), (FIRST, PIECE)]:
-            chunk = slice(last.start + lo, last.start + hi)
-            nc.vector.tensor_tensor(product[:, chunk], value[:, chunk], last_gate[:, lo:hi], ALU.mult)
-        for chunk in [slice(cut, last.start + FIRST), slice(last.start + FIRST, n)]:
-            nc.sync.dma_start(out[P:, chunk], product[:, chunk])
+
+        def store(lo, hi):
+            nc.sync.dma_start(out[P:, lo:hi], product[:, lo:hi])
+
+        def multiply_on_gpsimd(lo, hi):
+            nc.gpsimd.tensor_tensor(product[:, lo:hi], value[:, lo:hi], gate[:, lo:hi], ALU.mult)
+
+        def multiply_on_vector(lo, hi):
+            in_psum = moved_gate[:, lo - middle.start : hi - middle.start]
+            nc.vector.tensor_tensor(product[:, lo:hi], value[:, lo:hi], in_psum, ALU.mult)
+
+        for lo, hi in [(0, PIECE), (middle.start, cut)]:
+            multiply_on_gpsimd(lo, hi)
+            store(lo, hi)
+        for lo, hi in [(cut, last.start), (last.start, n - HALF), (n - HALF, n)]:
+            multiply_on_vector(lo, hi)
+            store(lo, hi)

@@ -11,7 +11,7 @@ PIECE = 512
 OFFSETS_PER_COLUMN = 16
 HALF = PIECE // 2
 BURST_BYTES = 256
-ON_GPSIMD = 320
+ON_GPSIMD = 256
 
 
 def tile_lookup_vg_nrmsilu_out_kernel(tc, tab, offs, out):

@@ -11,7 +11,9 @@ PIECE = 512
 OFFSETS_PER_COLUMN = 16
 HALF = PIECE // 2
 BURST_BYTES = 256
+EARLY = 192
 ON_GPSIMD = 256
+SHARED = 160
 
 
 def tile_lookup_vg_nrmsilu_out_kernel(tc, tab, offs, out):
@@ -67,15 +69,16 @@ def tile_lookup_vg_nrmsilu_out_kernel(tc, tab, offs, out):
 
         gate = look_up_gates(gate_table1, "gate1", [last, first, middle])
         cut = middle.start + ON_GPSIMD
+        shared = n - SHARED
         moved_gate = psum.tile([P, 2 * PIECE], F32, name="moved_gate")
-        for columns in [last, slice(cut, last.start)]:
-            into = moved_gate[:, columns.start - middle.start : columns.stop - middle.start]
-            nc.tensor.matmul(into, identity[:], gate[:, columns], start=True, stop=True)
+        for lo, hi in [(last.start, shared), (cut, last.start)]:
+            into = moved_gate[:, lo - middle.start : hi - middle.start]
+            nc.tensor.matmul(into, identity[:], gate[:, lo:hi], start=True, stop=True)
         value = look_up_values(value_table1, "value1", [first, middle, last])
         product = held.tile([P, n], F32, name="product1", align_bytes=BURST_BYTES)
 
-        def store(lo, hi):
-            nc.sync.dma_start(out[P:, lo:hi], product[:, lo:hi])
+        def store(queue, lo, hi):
+            queue.dma_start(out[P:, lo:hi], product[:, lo:hi])
 
         def multiply_on_gpsimd(lo, hi):
             nc.gpsimd.tensor_tensor(product[:, lo:hi], value[:, lo:hi], gate[:, lo:hi], ALU.mult)
@@ -86,7 +89,12 @@ def tile_lookup_vg_nrmsilu_out_kernel(tc, tab, offs, out):
 
         for lo, hi in [(0, PIECE), (middle.start, cut)]:
             multiply_on_gpsimd(lo, hi)
-            store(lo, hi)
-        for lo, hi in [(cut, last.start), (last.start, n - HALF), (n - HALF, n)]:
-            multiply_on_vector(lo, hi)
-            store(lo, hi)
+            store(nc.sync, lo, hi)
+        multiply_on_vector(cut, last.start)
+        store(nc.sync, cut, last.start)
+        early = last.start + EARLY
+        multiply_on_vector(last.start, early)
+        store(nc.scalar, last.start, early)
+        multiply_on_vector(early, shared)
+        multiply_on_gpsimd(shared, n)
+        store(nc.sync, early, n)

@@ -77,8 +77,8 @@ def tile_lookup_vg_nrmsilu_out_kernel(tc, tab, offs, out):
         value = look_up_values(value_table1, "value1", [first, middle, last])
         product = held.tile([P, n], F32, name="product1", align_bytes=BURST_BYTES)
 
-        def store(queue, lo, hi):
-            queue.dma_start(out[P:, lo:hi], product[:, lo:hi])
+        def store(lo, hi):
+            nc.sync.dma_start(out[P:, lo:hi], product[:, lo:hi])
 
         def multiply_on_gpsimd(lo, hi):
             nc.gpsimd.tensor_tensor(product[:, lo:hi], value[:, lo:hi], gate[:, lo:hi], ALU.mult)
@@ -89,12 +89,12 @@ def tile_lookup_vg_nrmsilu_out_kernel(tc, tab, offs, out):
 
         for lo, hi in [(0, PIECE), (middle.start, cut)]:
             multiply_on_gpsimd(lo, hi)
-            store(nc.sync, lo, hi)
+            store(lo, hi)
         multiply_on_vector(cut, last.start)
-        store(nc.sync, cut, last.start)
+        store(cut, last.start)
         early = last.start + EARLY
         multiply_on_vector(last.start, early)
-        store(nc.scalar, last.start, early)
+        store(last.start, early)
         multiply_on_vector(early, shared)
         multiply_on_gpsimd(shared, n)
-        store(nc.sync, early, n)
+        store(early, n)

import concourse.mybir as mybir
from concourse.masks import make_identity

F32 = mybir.dt.float32
U16 = mybir.dt.uint16
ALU = mybir.AluOpType
SILU = mybir.ActivationFunctionType.Silu

P = 128
PIECE = 512
OFFSETS_PER_COLUMN = 16
HALF = PIECE // 2
BURST_BYTES = 256
EARLY = 192
ON_GPSIMD = 256
SHARED = 160


def tile_lookup_vg_nrmsilu_out_kernel(tc, tab, offs, out):
    nc = tc.nc
    places = tab.shape[2]
    n = out.shape[1]
    first, middle, last = [slice(lo, lo + PIECE) for lo in range(0, n, PIECE)]

    with tc.tile_pool(name="held", bufs=1) as held, tc.psum_pool(name="psum", bufs=1) as psum:
        unused = held.tile([P, 1], F32, name="unused")
        nc.vector.memset(unused[:], 0.0)
        nc.scalar.activation(unused[:], unused[:], SILU)

        def load(which, block):
            table = held.tile([P, places], F32, name=f"table{which}_{block}", align_bytes=BURST_BYTES)
            nc.sync.dma_start(table[:], tab[which, block * P : (block + 1) * P, :])
            return table

        gate_table0 = load(1, 0)
        lists = held.tile([P, n // OFFSETS_PER_COLUMN], U16, name="lists", align_bytes=BURST_BYTES)
        nc.sync.dma_start(lists[:], offs)
        value_table0 = load(0, 0)
        gate_table1 = load(1, 1)
        value_table1 = load(0, 1)

        identity = held.tile([P, P], F32, name="identity")
        make_identity(nc, identity[:])

        def entries(piece):
            return lists[:, piece.start // OFFSETS_PER_COLUMN : piece.stop // OFFSETS_PER_COLUMN]

        def look_up_values(table, name, pieces):
            value = held.tile([P, n], F32, name=name)
            for piece in pieces:
                nc.vector.tensor_scalar(
                    value[:, piece], table[:].indirect(entries(piece)), 0.125, 1.5, ALU.subtract, ALU.mult
                )
            return value

        def look_up_gates(table, name, pieces):
            gate = held.tile([P, n], F32, name=name)
            for piece in pieces:
                nc.scalar.activation(gate[:, piece], table[:].indirect(entries(piece)), SILU)
            return gate

        gate = look_up_gates(gate_table0, "gate0", [first, middle, last])
        value = look_up_values(value_table0, "value0", [first, middle, last])
        product = held.tile([P, n], F32, name="product0", align_bytes=BURST_BYTES)
        for piece in [first, middle, last]:
            nc.gpsimd.tensor_tensor(product[:, piece], value[:, piece], gate[:, piece], ALU.mult)
        for lo in range(0, n, HALF):
            nc.sync.dma_start(out[:P, lo : lo + HALF], product[:, lo : lo + HALF])

        gate = look_up_gates(gate_table1, "gate1", [last, first, middle])
        cut = middle.start + ON_GPSIMD
        shared = n - SHARED
        moved_gate = psum.tile([P, 2 * PIECE], F32, name="moved_gate")
        for lo, hi in [(last.start, shared), (cut, last.start)]:
            into = moved_gate[:, lo - middle.start : hi - middle.start]
            nc.tensor.matmul(into, identity[:], gate[:, lo:hi], start=True, stop=True)
        value = look_up_values(value_table1, "value1", [first, middle, last])
        product = held.tile([P, n], F32, name="product1", align_bytes=BURST_BYTES)

        def store(lo, hi):
            nc.sync.dma_start(out[P:, lo:hi], product[:, lo:hi])

        def multiply_on_gpsimd(lo, hi):
            nc.gpsimd.tensor_tensor(product[:, lo:hi], value[:, lo:hi], gate[:, lo:hi], ALU.mult)

        def multiply_on_vector(lo, hi):
            in_psum = moved_gate[:, lo - middle.start : hi - middle.start]
            nc.vector.tensor_tensor(product[:, lo:hi], value[:, lo:hi], in_psum, ALU.mult)

        for lo, hi in [(0, PIECE), (middle.start, cut)]:
            multiply_on_gpsimd(lo, hi)
            store(lo, hi)
        multiply_on_vector(cut, last.start)
        store(cut, last.start)
        early = last.start + EARLY
        multiply_on_vector(last.start, early)
        store(last.start, early)
        multiply_on_vector(early, shared)
        multiply_on_gpsimd(shared, n)
        store(early, n)
